import numpy as np
import ml_dtypes


def mxq(x, axis, fmt="e4m3"):
    dtype, down = {"e4m3": (ml_dtypes.float8_e4m3fn, 7), "e5m2": (ml_dtypes.float8_e5m2, 14)}[fmt]
    v = np.moveaxis(np.asarray(x, np.float32).astype(ml_dtypes.bfloat16).astype(np.float64), axis, -1)
    blocks = v.reshape(v.shape[:-1] + (-1, 32))
    amax = np.abs(blocks).max(-1, keepdims=True)
    byte = np.maximum(np.where(amax > 0, np.frexp(amax)[1] - 1 + 127, 0) - down, 1)
    scale = np.exp2(byte - 127.0)
    codes = (blocks / scale).astype(np.float32).astype(dtype).astype(np.float64)
    return np.moveaxis((codes * scale).reshape(v.shape), -1, axis)


WIDE = False


def mx_kscale(k):
    if not WIDE:
        return np.ones(k)
    levels = np.array([10, -10, 5, -5, 0])
    if k % 512:
        return np.exp2(np.random.permutation(np.resize(levels, k // 32))).repeat(32)
    a = np.empty((k // 512, 16))
    for p in range(k // 512):
        a[p, :8] = np.random.permutation(np.resize(levels, 8))
        for g in range(8):
            far = levels[np.abs(levels - a[p, g]) >= 10]
            a[p, g + 8] = far[np.random.randint(len(far))]
    return np.exp2(a.ravel()).repeat(32)


def f64(x):
    return np.asarray(x).astype(np.float64)


def striped(idx):
    return np.tile(idx.reshape(-1, 16).T, (8, 1)).astype(np.uint16)


def unstriped(offs):
    return offs[:16].T.reshape(-1).astype(np.int64)


def striped8(idx):
    return np.concatenate([x.reshape(-1, 16).T for x in idx]).astype(np.uint16)


def runs(offs, k):
    lists = np.stack([offs[16 * r : 16 * r + 16].T.reshape(-1) for r in range(8)]).astype(np.int64)
    return lists[np.arange(k) % 512 // 64]


def pack_weight(w):
    k, n = w.shape
    w = f64(np.asarray(w, np.float32).astype(ml_dtypes.bfloat16)).reshape(k // 32, 32, n)
    amax = np.abs(w).max(1)
    byte = np.clip(np.where(amax > 0, np.frexp(amax)[1] - 1 + 127 - 7, 1), 1, 254)
    scaled = (w * np.exp2(127.0 - byte)[:, None, :]).reshape(k, n).astype(np.float32)
    words = np.ascontiguousarray(scaled.reshape(k // 512, 128, 4, n).transpose(0, 1, 3, 2)).astype(ml_dtypes.float8_e4m3fn).view(np.uint8)
    return words, np.ascontiguousarray(byte.astype(np.uint8).reshape(k // 512, 16, n))


def unpack_weight(words, scales):
    g, p, n, _ = words.shape
    vals = np.ascontiguousarray(words).view(ml_dtypes.float8_e4m3fn).astype(np.float64) * np.repeat(np.exp2(scales.astype(np.float64) - 127.0), 8, axis=1)[..., None]
    return vals.transpose(0, 1, 3, 2).reshape(g * 512, n)


def sigmoid(v):
    return 1.0 / (1.0 + np.exp(-np.maximum(v, -700.0)))


K, T, S, N, H, G = 512, 2048, 512, 512, 512, 2048


def setup_inputs():
    n = np.random.standard_normal
    s = mx_kscale(K)[:, None]
    u = mx_kscale(S)
    packed_xT = pack_weight(n((K, T)) * s)
    packed_dT = pack_weight(n((K, G)) / s)
    return {
        "x_words": packed_xT[0],
        "x_scales": packed_xT[1],
        "w1": (n((K, H)) / np.sqrt(K) / s).astype(np.float32),
        "gn": (np.random.uniform(0.5, 1.5, (H, 1)) * u[:, None]).astype(np.float32),
        "w2": (n((H, N)) / np.sqrt(H) / u[:, None]).astype(np.float32),
        "d_words": packed_dT[0],
        "d_scales": packed_dT[1],
        "offs": striped(np.random.permutation(T)[:S]),
        "n1": striped8(np.stack([np.random.permutation(S) for _ in range(8)])),
        "two": striped(np.random.permutation(T)[:S]),
        "k1": striped8(np.random.randint(0, G, (8, H))),
        "n2": striped8(np.stack([np.random.permutation(S) for _ in range(8)])),
        "n3": striped8(np.stack([np.random.permutation(S) for _ in range(8)])),
    }


def reference(x_words, x_scales, w1, gn, w2, d_words, d_scales, offs, n1, two, k1, n2, n3):
    xq = unpack_weight(x_words, x_scales)[:, unstriped(offs)]
    y = mxq(f64(w1), 0, "e4m3").T @ xq
    z = f64(gn) * (y * (sigmoid(y[np.arange(H)[:, None], runs(n1, H)])))
    a = mxq(f64(w2), 0, "e4m3").T @ mxq(z, 0, "e4m3")
    d_k1 = unpack_weight(d_words, d_scales)[np.arange(K)[:, None], runs(k1, K)]
    x_two = unpack_weight(x_words, x_scales)[:, unstriped(two)]
    b = 0.0625 * (d_k1.T @ x_two)
    return (a + a[np.arange(N)[:, None], runs(n2, N)]) * (sigmoid(b + b[np.arange(H)[:, None], runs(n3, H)]))

@@ -1,0 +1,230 @@
+from contextlib import ExitStack
+
+import concourse.mybir as mybir
+from concourse.masks import make_identity
+
+F32 = mybir.dt.float32
+BF16 = mybir.dt.bfloat16
+I32 = mybir.dt.int32
+U32 = mybir.dt.uint32
+U16 = mybir.dt.uint16
+U8 = mybir.dt.uint8
+FP8X4 = mybir.dt.float8_e4m3fn_x4
+ACT = mybir.ActivationFunctionType
+ALU = mybir.AluOpType
+
+P = 128
+PACK = 4
+T = 2048
+S = 512
+HALF = S // 2
+FLOPS = 3 * 2 * 512 * 512 * 512
+
+
+def tile_picked_cdjointriebgate_none_p_kernel(tc, x_words, x_scales, w1, gn, w2, d_words, d_scales, offs, n1, two, k1, n2, n3, out):
+    nc = tc.nc
+    with ExitStack() as ctx:
+        keep = ctx.enter_context(tc.tile_pool(name="keep", bufs=1))
+        shared = ctx.enter_context(tc.tile_pool(name="shared", bufs=1))
+        psum = ctx.enter_context(tc.psum_pool(name="psum", bufs=1))
+
+        def sb(name, shape, dtype, tag=None):
+            return keep.tile(shape, dtype, name=name, tag=tag or name, align_bytes=64)
+
+        def placed(name, shape, dtype, offset):
+            return shared.tile(shape, dtype, name=name, align_bytes=64, offset=offset)
+
+        def bank(tag, name):
+            return psum.tile([P, S], F32, name=name, tag=tag)
+
+        lists = {name: sb(name + "_list", [P, S // 16], U16) for name in ("offs", "n1", "two", "k1", "n2", "n3")}
+        x_tab = sb("x_tab", [P, T], U32)
+        xs_tab = sb("xs_tab", [P, T], U8)
+        ds_tab = sb("ds_tab", [P, T], U8)
+        w1_raw = [sb(f"w1_raw{h}", [P, PACK, HALF], F32) for h in range(2)]
+        gain = sb("gain", [P, PACK], F32)
+
+        w1_rows = w1.rearrange("(p j) c -> p j c", j=PACK)
+        xs_rows = x_scales[0].bitcast(I32)
+        ds_rows = d_scales[0].bitcast(I32)
+
+        nc.vector.memset(xs_tab[:].bitcast(I32), 0)
+        nc.gpsimd.memset(ds_tab[:].bitcast(I32), 0)
+        for i in range(2):
+            nc.gpsimd.dma_start(ds_tab[:].bitcast(I32)[i:P:16, :], ds_rows[i:16:2, :])
+        nc.gpsimd.dma_start(gain[:], gn.rearrange("(p t) o -> p (t o)", t=PACK))
+        for name, src in (("k1", k1), ("offs", offs), ("two", two), ("n1", n1), ("n3", n3), ("n2", n2)):
+            nc.sync.dma_start(lists[name][:], src)
+        for h in range(2):
+            nc.sync.dma_start(w1_raw[h][:], w1_rows[:, :, h * HALF:(h + 1) * HALF])
+        nc.sync.dma_start(x_tab[:].bitcast(I32), x_words[0].rearrange("p n r -> p (n r)").bitcast(I32))
+        d_tab = sb("d_tab", [P, T], U32)
+        nc.sync.dma_start(d_tab[:].bitcast(I32), d_words[0].rearrange("p n r -> p (n r)").bitcast(I32))
+        for i in range(4):
+            nc.scalar.dma_start(xs_tab[:].bitcast(I32)[i:P:32, :], xs_rows[i:16:4, :])
+
+        def pick(name, table, which, dtype, tag=None, offset=None):
+            picked = sb(name, [P, S], dtype, tag) if offset is None else placed(name, [P, S], dtype, offset)
+            nc.vector.tensor_copy(picked[:], table[:].indirect(lists[which][:]))
+            return picked
+
+        def dealt(grouped):
+            return grouped[:].rearrange("p (t m j) -> p m j t", t=PACK, j=PACK)
+
+        def quantize(name, grouped, pieces):
+            codes = sb(name + "_codes", [P, S], U32)
+            scales = sb(name + "_scales", [P, S], U8)
+
+            def piece(i):
+                w = S // pieces
+                nc.vector.quantize_mx(out=codes[:, i * w:(i + 1) * w].bitcast(FP8X4), scales=scales[:, i * w:(i + 1) * w],
+                                      in_=grouped[:, PACK * i * w:PACK * (i + 1) * w])
+            return codes, scales, piece
+
+        def product(acc, t, stat, stat_s, mov, mov_s):
+            cols = slice(t * P, (t + 1) * P)
+            nc.tensor.matmul_mx(out=acc[:], lhsT=stat[:, cols].bitcast(FP8X4), lhsT_scale=stat_s[:, cols],
+                                rhs=mov[:].bitcast(FP8X4), rhs_scale=mov_s[:], start=True, stop=True)
+
+        def fetch(engine, dst, window, which, h):
+            src = window[:].indirect(lists[which][:, h * HALF // 16:(h + 1) * HALF // 16])
+            cols = slice(h * HALF, (h + 1) * HALF)
+            if engine == "V":
+                nc.vector.tensor_copy(dst[:, cols], src)
+            else:
+                nc.scalar.activation(dst[:, cols], src, ACT.Copy)
+
+        def scaled_copy(engine, dst, src, factor):
+            if engine == "V":
+                nc.vector.tensor_scalar(dst, src, factor, None, ALU.mult)
+            else:
+                nc.scalar.activation(dst, src, ACT.Copy, scale=factor)
+
+        w1_grouped = placed("w1_grouped", [P, PACK * S], BF16, 1024)
+        for h in range(2):
+            nc.scalar.copy(dealt(w1_grouped)[:, h * 64:(h + 1) * 64], w1_raw[h][:].rearrange("p j (m t) -> p m j t", t=PACK))
+        w2_raw = sb("w2_raw", [P, PACK, S], F32, tag="w1_raw1")
+        nc.sync.dma_start(w2_raw[:], w2.rearrange("(p j) c -> p j c", j=PACK))
+        ds_k1 = pick("ds_k1", ds_tab, "k1", U8)
+        ds_dealt = sb("ds_dealt", [P, S], U8)
+        nc.vector.tensor_copy(ds_dealt[:].rearrange("p (t m) -> p m t", t=PACK), ds_k1[:].rearrange("p (m t) -> p m t", t=PACK))
+        for i in range(2):
+            nc.sync.dma_start(ds_dealt[:].bitcast(I32)[2 + i:P:32, :], ds_dealt[:].bitcast(I32)[16 + i:P:32, :])
+        xs_offs = pick("xs_offs", xs_tab, "offs", U8, tag="ds_k1")
+        ident = sb("ident", [P, P], F32, tag="ds_tab")
+        make_identity(nc, ident[:])
+        w1_codes, w1_scales, w1_piece = quantize("w1", w1_grouped, 2)
+        w1_piece(0)
+        w1_piece(1)
+        x_offs = pick("x_offs", x_tab, "offs", U32, offset=0)
+
+        y_bank = [bank(f"ya{t}", f"y{t}") for t in range(PACK)]
+        gate = [sb(f"gate{t}", [P, S], F32) for t in range(PACK)]
+        gate_n1 = [sb(f"gate_n1_{t}", [P, S], F32) for t in range(PACK)]
+        for t in range(PACK):
+            product(y_bank[t], t, w1_codes, w1_scales, x_offs, xs_offs)
+        for t in range(PACK):
+            nc.scalar.activation(gate[t][:], y_bank[t][:], ACT.Sigmoid)
+        xs_two = pick("xs_two", xs_tab, "two", U8, offset=2048)
+        x_two = pick("x_two", x_tab, "two", U32, offset=2560)
+        d_k1 = pick("d_k1", d_tab, "k1", U32, offset=4608)
+        d_dealt = sb("d_dealt", [P, S], U32)
+        nc.vector.tensor_copy(d_dealt[:].rearrange("p (t c i) -> p c t i", t=PACK, i=4), d_k1[:].rearrange("p (c i t) -> p c t i", t=PACK, i=4))
+        b_bank = [bank(f"b{t}", f"b{t}") for t in range(PACK)]
+        for t in range(PACK):
+            product(b_bank[t], t, d_dealt, ds_dealt, x_two, xs_two)
+
+        w2_grouped = sb("w2_grouped", [P, PACK * S], BF16)
+        nc.vector.tensor_copy(dealt(w2_grouped), w2_raw[:].rearrange("p j (m t) -> p m j t", t=PACK))
+
+        z_rows = sb("z_rows", [P, PACK, S], BF16)
+        z_grouped = sb("z_grouped", [P, PACK * S], BF16)
+        z_codes, z_scales, z_piece = quantize("z", z_grouped, 2)
+        w2_codes, w2_scales, w2_piece = quantize("w2", w2_grouped, 1)
+        for h in range(2):
+            cols = slice(h * HALF, (h + 1) * HALF)
+            for t in range(PACK):
+                fetch("S", gate_n1[t], gate[t], "n1", h)
+            for t in range(PACK):
+                nc.vector.scalar_tensor_tensor(z_rows[:, t, cols], y_bank[t][:, cols], gain[:, t:t + 1], gate_n1[t][:, cols], ALU.mult, ALU.mult)
+            nc.vector.tensor_copy(
+                z_grouped[:, PACK * h * HALF:PACK * (h + 1) * HALF].rearrange("p (c i t) -> p c t i", t=PACK, i=4),
+                z_rows[:, :, cols].rearrange("p t (c i) -> p c t i", i=4))
+            if h == 0:
+                w2_piece(0)
+            z_piece(h)
+
+        b_rows = [sb(f"b_rows{t}", [P, S], F32) for t in range(PACK)]
+        b_n3 = [sb(f"b_n3_{t}", [P, S], F32) for t in range(PACK)]
+        s_turned = [sb(f"s_turned{t}", [P, S], F32) for t in range(PACK)]
+        sum_bank = [None] * PACK
+        s_bank = [None] * PACK
+        a_rows = [sb(f"a_rows{t}", [P, S], F32) for t in range(PACK)]
+        a_n2 = [sb(f"a_n2_{t}", [P, S], F32) for t in range(PACK)]
+        a_sum = [sb(f"a_sum{t}", [P, S], F32) for t in range(PACK)]
+        res = [sb(f"res{t}", [P, S], F32) for t in range(PACK)]
+        out_rows = out.rearrange("(p t) j -> p t j", t=PACK)
+
+        def b_fetch(t, engine):
+            for h in range(2):
+                fetch(engine, b_n3[t], b_rows[t], "n3", h)
+            sum_bank[t] = bank(f"b{t}", f"bsum{t}")
+            for c in range(PACK):
+                cols = slice(c * P, (c + 1) * P)
+                nc.tensor.matmul(sum_bank[t][:, cols], b_rows[t][:, cols], ident[:], start=True, stop=False, is_transpose=True)
+                nc.tensor.matmul(sum_bank[t][:, cols], b_n3[t][:, cols], ident[:], start=False, stop=True, is_transpose=True)
+
+        def b_gate(t):
+            nc.scalar.activation(s_turned[t][:], sum_bank[t][:], ACT.Sigmoid)
+            s_bank[t] = bank(f"b{t}", f"s{t}")
+            for c in range(PACK):
+                cols = slice(c * P, (c + 1) * P)
+                nc.tensor.transpose(s_bank[t][:, cols], s_turned[t][:, cols], ident[:])
+
+        def a_copy(t, engine):
+            if engine == "V":
+                nc.vector.tensor_copy(a_rows[t][:], a_bank[t][:])
+            else:
+                nc.scalar.copy(a_rows[t][:], a_bank[t][:])
+
+        def a_fetch(t, engine):
+            for h in range(2):
+                fetch(engine, a_n2[t], a_rows[t], "n2", h)
+
+        def add(t):
+            nc.vector.tensor_tensor(a_sum[t][:], a_bank[t][:], a_n2[t][:], ALU.add)
+
+        def finish(t):
+            nc.vector.tensor_tensor(res[t][:], s_bank[t][:], a_sum[t][:], ALU.mult)
+            nc.sync.dma_start(out_rows[:, t, :], res[t][:])
+
+        for t in range(PACK):
+            scaled_copy("S", b_rows[t][:], b_bank[t][:], 0.0625)
+        a_bank = [bank(f"ya{t}", f"a{t}") for t in range(PACK)]
+        for t in range(PACK):
+            product(a_bank[t], t, w2_codes, w2_scales, z_codes, z_scales)
+        b_fetch(0, "S")
+        b_fetch(1, "V")
+        a_copy(1, "S")
+        a_copy(0, "V")
+        b_fetch(2, "S")
+        a_fetch(0, "V")
+        b_gate(0)
+        add(0)
+        b_gate(1)
+        a_fetch(1, "V")
+        b_fetch(3, "S")
+        finish(0)
+        b_gate(2)
+        add(1)
+        a_copy(2, "S")
+        finish(1)
+        a_copy(3, "V")
+        a_fetch(2, "S")
+        fetch("V", a_n2[3], a_rows[3], "n2", 1)
+        b_gate(3)
+        add(2)
+        fetch("S", a_n2[3], a_rows[3], "n2", 0)
+        finish(2)
+        add(3)
+        finish(3)

@@ -1,7 +1,6 @@
 from contextlib import ExitStack
 
 import concourse.mybir as mybir
-from concourse.masks import make_identity
 
 F32 = mybir.dt.float32
 BF16 = mybir.dt.bfloat16
@@ -38,30 +37,29 @@ def tile_picked_cdjointriebgate_none_p_kernel(tc, x_words, x_scales, w1, gn, w2,
             return psum.tile([P, S], F32, name=name, tag=tag)
 
         lists = {name: sb(name + "_list", [P, S // 16], U16) for name in ("offs", "n1", "two", "k1", "n2", "n3")}
-        x_tab = sb("x_tab", [P, T], U32)
         xs_tab = sb("xs_tab", [P, T], U8)
         ds_tab = sb("ds_tab", [P, T], U8)
-        w1_raw = [sb(f"w1_raw{h}", [P, PACK, HALF], F32) for h in range(2)]
-        gain = sb("gain", [P, PACK], F32)
+        w1_raw = [placed(f"w1_raw{h}", [P, PACK, HALF], F32, 32768 + 16384 * h) for h in range(2)]
 
         w1_rows = w1.rearrange("(p j) c -> p j c", j=PACK)
         xs_rows = x_scales[0].bitcast(I32)
         ds_rows = d_scales[0].bitcast(I32)
 
+        ones = placed("ones", [P, P], F32, 8192 - 256)
+        ident = sb("ident", [P, P], F32)
         nc.vector.memset(xs_tab[:].bitcast(I32), 0)
-        nc.gpsimd.memset(ds_tab[:].bitcast(I32), 0)
-        for i in range(2):
-            nc.gpsimd.dma_start(ds_tab[:].bitcast(I32)[i:P:16, :], ds_rows[i:16:2, :])
-        nc.gpsimd.dma_start(gain[:], gn.rearrange("(p t) o -> p (t o)", t=PACK))
-        for name, src in (("k1", k1), ("offs", offs), ("two", two), ("n1", n1), ("n3", n3), ("n2", n2)):
+        nc.gpsimd.memset(ones[:], 1.0)
+        nc.gpsimd.affine_select(out=ident[:], in_=ones[:], compare_op=ALU.is_equal, fill=0.0, base=0, pattern=[[-1, P]], channel_multiplier=1)
+        nc.vector.memset(ds_tab[:].bitcast(I32), 0)
+        nc.gpsimd.dma_start(ds_tab[:].bitcast(I32)[0:P:8, :], ds_rows)
+        for name, src in (("offs", offs), ("k1", k1), ("two", two), ("n1", n1), ("n3", n3), ("n2", n2)):
             nc.sync.dma_start(lists[name][:], src)
         for h in range(2):
             nc.sync.dma_start(w1_raw[h][:], w1_rows[:, :, h * HALF:(h + 1) * HALF])
-        nc.sync.dma_start(x_tab[:].bitcast(I32), x_words[0].rearrange("p n r -> p (n r)").bitcast(I32))
-        d_tab = sb("d_tab", [P, T], U32)
-        nc.sync.dma_start(d_tab[:].bitcast(I32), d_words[0].rearrange("p n r -> p (n r)").bitcast(I32))
         for i in range(4):
-            nc.scalar.dma_start(xs_tab[:].bitcast(I32)[i:P:32, :], xs_rows[i:16:4, :])
+            nc.sync.dma_start(xs_tab[:].bitcast(I32)[i:P:32, :], xs_rows[i:16:4, :])
+        x_tab = placed("x_tab", [P, T], U32, 0)
+        nc.sync.dma_start(x_tab[:].bitcast(I32), x_words[0].rearrange("p n r -> p (n r)").bitcast(I32))
 
         def pick(name, table, which, dtype, tag=None, offset=None):
             picked = sb(name, [P, S], dtype, tag) if offset is None else placed(name, [P, S], dtype, offset)
@@ -86,9 +84,8 @@ def tile_picked_cdjointriebgate_none_p_kernel(tc, x_words, x_scales, w1, gn, w2,
             nc.tensor.matmul_mx(out=acc[:], lhsT=stat[:, cols].bitcast(FP8X4), lhsT_scale=stat_s[:, cols],
                                 rhs=mov[:].bitcast(FP8X4), rhs_scale=mov_s[:], start=True, stop=True)
 
-        def fetch(engine, dst, window, which, h):
-            src = window[:].indirect(lists[which][:, h * HALF // 16:(h + 1) * HALF // 16])
-            cols = slice(h * HALF, (h + 1) * HALF)
+        def fetch(engine, dst, window, which, cols=slice(0, S)):
+            src = window[:].indirect(lists[which][:, cols.start // 16:cols.stop // 16])
             if engine == "V":
                 nc.vector.tensor_copy(dst[:, cols], src)
             else:
@@ -100,79 +97,88 @@ def tile_picked_cdjointriebgate_none_p_kernel(tc, x_words, x_scales, w1, gn, w2,
             else:
                 nc.scalar.activation(dst, src, ACT.Copy, scale=factor)
 
-        w1_grouped = placed("w1_grouped", [P, PACK * S], BF16, 1024)
-        for h in range(2):
-            nc.scalar.copy(dealt(w1_grouped)[:, h * 64:(h + 1) * 64], w1_raw[h][:].rearrange("p j (m t) -> p m j t", t=PACK))
-        w2_raw = sb("w2_raw", [P, PACK, S], F32, tag="w1_raw1")
+        base = 16384
+        w1_grouped = placed("w1_grouped", [P, PACK * S], BF16, base + 1536)
+        w1_views = [w1_raw[h][:].rearrange("p j (m t) -> p m j t", t=PACK) for h in range(2)]
+        nc.scalar.copy(dealt(w1_grouped)[:, 0:64], w1_views[0])
+        d_tab = placed("d_tab", [P, T], U32, 32768 + 64)
+        nc.sync.dma_start(d_tab[:].bitcast(I32), d_words[0].rearrange("p n r -> p (n r)").bitcast(I32))
+        gain = placed("gain", [P, PACK], F32, 32768)
+        nc.sync.dma_start(gain[:], gn.rearrange("(p t) o -> p (t o)", t=PACK))
+        nc.scalar.copy(dealt(w1_grouped)[:, 64:128], w1_views[1])
+        w2_raw = placed("w2_raw", [P, PACK, S], F32, 32768 + 16384)
         nc.sync.dma_start(w2_raw[:], w2.rearrange("(p j) c -> p j c", j=PACK))
-        ds_k1 = pick("ds_k1", ds_tab, "k1", U8)
-        ds_dealt = sb("ds_dealt", [P, S], U8)
-        nc.vector.tensor_copy(ds_dealt[:].rearrange("p (t m) -> p m t", t=PACK), ds_k1[:].rearrange("p (m t) -> p m t", t=PACK))
-        for i in range(2):
-            nc.sync.dma_start(ds_dealt[:].bitcast(I32)[2 + i:P:32, :], ds_dealt[:].bitcast(I32)[16 + i:P:32, :])
-        xs_offs = pick("xs_offs", xs_tab, "offs", U8, tag="ds_k1")
-        ident = sb("ident", [P, P], F32, tag="ds_tab")
-        make_identity(nc, ident[:])
-        w1_codes, w1_scales, w1_piece = quantize("w1", w1_grouped, 2)
+        xs_offs = pick("xs_offs", xs_tab, "offs", U8)
+        w1_codes, w1_scales, w1_piece = quantize("w1", w1_grouped, 1)
         w1_piece(0)
-        w1_piece(1)
-        x_offs = pick("x_offs", x_tab, "offs", U32, offset=0)
-
+        xs_two = pick("xs_two", xs_tab, "two", U8, offset=base + 2048)
+        x_offs = pick("x_offs", x_tab, "offs", U32, offset=base)
         y_bank = [bank(f"ya{t}", f"y{t}") for t in range(PACK)]
-        gate = [sb(f"gate{t}", [P, S], F32) for t in range(PACK)]
+        gate_win = [sb(f"gate_win{t}", [P, 2 * S], F32) for t in range(PACK)]
+        b_win = [sb(f"b_win{t}", [P, 2 * S], F32) for t in range(PACK)]
+        a_win = [sb(f"a_win{t}", [P, 2 * S], F32) for t in range(PACK)]
+        gate = [w[:, :S] for w in gate_win]
         gate_n1 = [sb(f"gate_n1_{t}", [P, S], F32) for t in range(PACK)]
+        b_rows = [w[:, :S] for w in b_win]
+        a_rows = [w[:, :S] for w in a_win]
         for t in range(PACK):
             product(y_bank[t], t, w1_codes, w1_scales, x_offs, xs_offs)
         for t in range(PACK):
-            nc.scalar.activation(gate[t][:], y_bank[t][:], ACT.Sigmoid)
-        xs_two = pick("xs_two", xs_tab, "two", U8, offset=2048)
-        x_two = pick("x_two", x_tab, "two", U32, offset=2560)
-        d_k1 = pick("d_k1", d_tab, "k1", U32, offset=4608)
+            nc.scalar.activation(gate[t], y_bank[t][:], ACT.Sigmoid)
+        x_two = pick("x_two", x_tab, "two", U32, offset=base + 3072)
+        ds_k1 = pick("ds_k1", ds_tab, "k1", U8, tag="xs_offs")
+        ds_dealt = sb("ds_dealt", [P, S], U8)
+        nc.vector.tensor_copy(ds_dealt[:].rearrange("p (t m) -> p t m", t=PACK), ds_k1[:].rearrange("p (m t) -> p t m", t=PACK))
+        for i in range(1, 4):
+            nc.sync.dma_start(ds_dealt[:].bitcast(I32)[i:P:32, :], ds_dealt[:].bitcast(I32)[8 * i:P:32, :])
+        d_k1 = pick("d_k1", d_tab, "k1", U32, offset=base + 5120)
         d_dealt = sb("d_dealt", [P, S], U32)
         nc.vector.tensor_copy(d_dealt[:].rearrange("p (t c i) -> p c t i", t=PACK, i=4), d_k1[:].rearrange("p (c i t) -> p c t i", t=PACK, i=4))
         b_bank = [bank(f"b{t}", f"b{t}") for t in range(PACK)]
         for t in range(PACK):
             product(b_bank[t], t, d_dealt, ds_dealt, x_two, xs_two)
 
-        w2_grouped = sb("w2_grouped", [P, PACK * S], BF16)
-        nc.vector.tensor_copy(dealt(w2_grouped), w2_raw[:].rearrange("p j (m t) -> p m j t", t=PACK))
+        late = 65536
+        w2_grouped = placed("w2_grouped", [P, PACK * S], BF16, late)
 
         z_rows = sb("z_rows", [P, PACK, S], BF16)
-        z_grouped = sb("z_grouped", [P, PACK * S], BF16)
-        z_codes, z_scales, z_piece = quantize("z", z_grouped, 2)
+        z_grouped = placed("z_grouped", [P, PACK * S], BF16, late + 4096)
+        z_codes, z_scales, z_piece = quantize("z", z_grouped, 1)
         w2_codes, w2_scales, w2_piece = quantize("w2", w2_grouped, 1)
-        for h in range(2):
-            cols = slice(h * HALF, (h + 1) * HALF)
-            for t in range(PACK):
-                fetch("S", gate_n1[t], gate[t], "n1", h)
-            for t in range(PACK):
-                nc.vector.scalar_tensor_tensor(z_rows[:, t, cols], y_bank[t][:, cols], gain[:, t:t + 1], gate_n1[t][:, cols], ALU.mult, ALU.mult)
-            nc.vector.tensor_copy(
-                z_grouped[:, PACK * h * HALF:PACK * (h + 1) * HALF].rearrange("p (c i t) -> p c t i", t=PACK, i=4),
-                z_rows[:, :, cols].rearrange("p t (c i) -> p c t i", i=4))
-            if h == 0:
-                w2_piece(0)
-            z_piece(h)
+        for t in range(PACK):
+            fetch("S", gate_n1[t], gate_win[t], "n1")
+        for t in range(PACK):
+            nc.vector.scalar_tensor_tensor(z_rows[:, t, :], y_bank[t][:], gain[:, t:t + 1], gate_n1[t][:], ALU.mult, ALU.mult)
+            if t == 1:
+                nc.vector.tensor_copy(dealt(w2_grouped), w2_raw[:].rearrange("p j (m t) -> p m j t", t=PACK))
+        nc.vector.tensor_copy(
+            z_grouped[:].rearrange("p (c i t) -> p c t i", t=PACK, i=4),
+            z_rows[:].rearrange("p t (c i) -> p c t i", i=4))
+        w2_piece(0)
+        z_piece(0)
 
-        b_rows = [sb(f"b_rows{t}", [P, S], F32) for t in range(PACK)]
-        b_n3 = [sb(f"b_n3_{t}", [P, S], F32) for t in range(PACK)]
         s_turned = [sb(f"s_turned{t}", [P, S], F32) for t in range(PACK)]
         sum_bank = [None] * PACK
         s_bank = [None] * PACK
-        a_rows = [sb(f"a_rows{t}", [P, S], F32) for t in range(PACK)]
-        a_n2 = [sb(f"a_n2_{t}", [P, S], F32) for t in range(PACK)]
+        spot = [late, late + 4096, late + 2048, late]
+        b_n3 = [placed(f"b_n3_{t}", [P, S], F32, spot[t]) for t in range(PACK)]
+        a_n2 = [placed(f"a_n2_{t}", [P, S], F32, spot[t] if t else late + 8192) for t in range(PACK)]
         a_sum = [sb(f"a_sum{t}", [P, S], F32) for t in range(PACK)]
         res = [sb(f"res{t}", [P, S], F32) for t in range(PACK)]
         out_rows = out.rearrange("(p t) j -> p t j", t=PACK)
 
-        def b_fetch(t, engine):
-            for h in range(2):
-                fetch(engine, b_n3[t], b_rows[t], "n3", h)
+        def b_copy(t):
+            nc.scalar.activation(b_rows[t], b_bank[t][:], ACT.Copy, scale=0.0625)
             sum_bank[t] = bank(f"b{t}", f"bsum{t}")
             for c in range(PACK):
                 cols = slice(c * P, (c + 1) * P)
-                nc.tensor.matmul(sum_bank[t][:, cols], b_rows[t][:, cols], ident[:], start=True, stop=False, is_transpose=True)
-                nc.tensor.matmul(sum_bank[t][:, cols], b_n3[t][:, cols], ident[:], start=False, stop=True, is_transpose=True)
+                nc.tensor.matmul(sum_bank[t][:, cols], b_rows[t][:, cols], ident[:], start=(c == 0), stop=False, is_transpose=True)
+
+        def b_fetch(t, engine):
+            fetch(engine, b_n3[t], b_win[t], "n3")
+            for c in range(PACK):
+                cols = slice(c * P, (c + 1) * P)
+                nc.tensor.matmul(sum_bank[t][:, cols], b_n3[t][:, cols], ident[:], start=False, stop=(c == PACK - 1), is_transpose=True)
 
         def b_gate(t):
             nc.scalar.activation(s_turned[t][:], sum_bank[t][:], ACT.Sigmoid)
@@ -183,48 +189,50 @@ def tile_picked_cdjointriebgate_none_p_kernel(tc, x_words, x_scales, w1, gn, w2,
 
         def a_copy(t, engine):
             if engine == "V":
-                nc.vector.tensor_copy(a_rows[t][:], a_bank[t][:])
+                nc.vector.tensor_copy(a_rows[t], a_bank[t][:])
             else:
-                nc.scalar.copy(a_rows[t][:], a_bank[t][:])
+                nc.scalar.copy(a_rows[t], a_bank[t][:])
 
-        def a_fetch(t, engine):
-            for h in range(2):
-                fetch(engine, a_n2[t], a_rows[t], "n2", h)
+        def a_fetch(t, engine, cols=slice(0, S)):
+            fetch(engine, a_n2[t], a_win[t], "n2", cols)
 
-        def add(t):
-            nc.vector.tensor_tensor(a_sum[t][:], a_bank[t][:], a_n2[t][:], ALU.add)
+        def add(t, cols=slice(0, S)):
+            nc.vector.tensor_tensor(a_sum[t][:, cols], a_bank[t][:, cols], a_n2[t][:, cols], ALU.add)
 
-        def finish(t):
-            nc.vector.tensor_tensor(res[t][:], s_bank[t][:], a_sum[t][:], ALU.mult)
-            nc.sync.dma_start(out_rows[:, t, :], res[t][:])
+        def finish(t, cols=slice(0, S)):
+            nc.vector.tensor_tensor(res[t][:, cols], s_bank[t][:, cols], a_sum[t][:, cols], ALU.mult)
+            nc.sync.dma_start(out_rows[:, t, cols], res[t][:, cols])
 
         for t in range(PACK):
-            scaled_copy("S", b_rows[t][:], b_bank[t][:], 0.0625)
+            b_copy(t)
         a_bank = [bank(f"ya{t}", f"a{t}") for t in range(PACK)]
         for t in range(PACK):
             product(a_bank[t], t, w2_codes, w2_scales, z_codes, z_scales)
+        halves = [slice(h * HALF, (h + 1) * HALF) for h in range(2)]
         b_fetch(0, "S")
         b_fetch(1, "V")
-        a_copy(1, "S")
-        a_copy(0, "V")
         b_fetch(2, "S")
+        a_copy(0, "V")
         a_fetch(0, "V")
         b_gate(0)
+        a_copy(1, "V")
         add(0)
-        b_gate(1)
-        a_fetch(1, "V")
         b_fetch(3, "S")
+        a_copy(2, "V")
         finish(0)
-        b_gate(2)
-        add(1)
-        a_copy(2, "S")
-        finish(1)
+        b_gate(1)
+        a_fetch(1, "S")
         a_copy(3, "V")
-        a_fetch(2, "S")
-        fetch("V", a_n2[3], a_rows[3], "n2", 1)
+        a_fetch(3, "V", halves[1])
+        b_gate(2)
         b_gate(3)
-        add(2)
-        fetch("S", a_n2[3], a_rows[3], "n2", 0)
-        finish(2)
+        add(1)
+        a_fetch(3, "S", halves[0])
+        finish(1)
         add(3)
+        for h in halves:
+            a_fetch(2, "S", h)
         finish(3)
+        for h in halves:
+            add(2, h)
+            finish(2, h)

@@ -48,16 +48,16 @@ def tile_picked_cdjointriebgate_none_p_kernel(tc, x_words, x_scales, w1, gn, w2,
         ones = placed("ones", [P, P], F32, 8192 - 256)
         ident = sb("ident", [P, P], F32)
         nc.vector.memset(xs_tab[:].bitcast(I32), 0)
+        nc.gpsimd.memset(ds_tab[:].bitcast(I32), 0)
         nc.gpsimd.memset(ones[:], 1.0)
         nc.gpsimd.affine_select(out=ident[:], in_=ones[:], compare_op=ALU.is_equal, fill=0.0, base=0, pattern=[[-1, P]], channel_multiplier=1)
-        nc.vector.memset(ds_tab[:].bitcast(I32), 0)
-        nc.gpsimd.dma_start(ds_tab[:].bitcast(I32)[0:P:8, :], ds_rows)
         for name, src in (("offs", offs), ("k1", k1), ("two", two), ("n1", n1), ("n3", n3), ("n2", n2)):
             nc.sync.dma_start(lists[name][:], src)
         for h in range(2):
             nc.sync.dma_start(w1_raw[h][:], w1_rows[:, :, h * HALF:(h + 1) * HALF])
         for i in range(4):
             nc.sync.dma_start(xs_tab[:].bitcast(I32)[i:P:32, :], xs_rows[i:16:4, :])
+        nc.sync.dma_start(ds_tab[:].bitcast(I32)[0:P:8, :], ds_rows)
         x_tab = placed("x_tab", [P, T], U32, 0)
         nc.sync.dma_start(x_tab[:].bitcast(I32), x_words[0].rearrange("p n r -> p (n r)").bitcast(I32))
 
@@ -109,29 +109,28 @@ def tile_picked_cdjointriebgate_none_p_kernel(tc, x_words, x_scales, w1, gn, w2,
         w2_raw = placed("w2_raw", [P, PACK, S], F32, 32768 + 16384)
         nc.sync.dma_start(w2_raw[:], w2.rearrange("(p j) c -> p j c", j=PACK))
         xs_offs = pick("xs_offs", xs_tab, "offs", U8)
-        w1_codes, w1_scales, w1_piece = quantize("w1", w1_grouped, 1)
-        w1_piece(0)
-        xs_two = pick("xs_two", xs_tab, "two", U8, offset=base + 2048)
+        ds_k1 = pick("ds_k1", ds_tab, "k1", U8)
+        first = 57344
+        w1_codes = [placed("w1_codes0", [P, HALF], U32, first), sb("w1_codes1", [P, HALF], U32)]
+        w1_scales = [placed("w1_scales0", [P, HALF], U8, first + 1024), sb("w1_scales1", [P, HALF], U8)]
+        for h in range(2):
+            nc.vector.quantize_mx(out=w1_codes[h][:].bitcast(FP8X4), scales=w1_scales[h][:], in_=w1_grouped[:, h * 1024:(h + 1) * 1024])
         x_offs = pick("x_offs", x_tab, "offs", U32, offset=base)
         y_bank = [bank(f"ya{t}", f"y{t}") for t in range(PACK)]
         gate_win = [sb(f"gate_win{t}", [P, 2 * S], F32) for t in range(PACK)]
-        b_win = [sb(f"b_win{t}", [P, 2 * S], F32) for t in range(PACK)]
-        a_win = [sb(f"a_win{t}", [P, 2 * S], F32) for t in range(PACK)]
         gate = [w[:, :S] for w in gate_win]
         gate_n1 = [sb(f"gate_n1_{t}", [P, S], F32) for t in range(PACK)]
-        b_rows = [w[:, :S] for w in b_win]
-        a_rows = [w[:, :S] for w in a_win]
         for t in range(PACK):
-            product(y_bank[t], t, w1_codes, w1_scales, x_offs, xs_offs)
+            product(y_bank[t], t % 2, w1_codes[t // 2], w1_scales[t // 2], x_offs, xs_offs)
         for t in range(PACK):
             nc.scalar.activation(gate[t], y_bank[t][:], ACT.Sigmoid)
         x_two = pick("x_two", x_tab, "two", U32, offset=base + 3072)
-        ds_k1 = pick("ds_k1", ds_tab, "k1", U8, tag="xs_offs")
-        ds_dealt = sb("ds_dealt", [P, S], U8)
+        ds_dealt = placed("ds_dealt", [P, S], U8, first)
         nc.vector.tensor_copy(ds_dealt[:].rearrange("p (t m) -> p t m", t=PACK), ds_k1[:].rearrange("p (m t) -> p t m", t=PACK))
         for i in range(1, 4):
             nc.sync.dma_start(ds_dealt[:].bitcast(I32)[i:P:32, :], ds_dealt[:].bitcast(I32)[8 * i:P:32, :])
-        d_k1 = pick("d_k1", d_tab, "k1", U32, offset=base + 5120)
+        xs_two = pick("xs_two", xs_tab, "two", U8, offset=first + 512)
+        d_k1 = pick("d_k1", d_tab, "k1", U32, offset=first + 1024)
         d_dealt = sb("d_dealt", [P, S], U32)
         nc.vector.tensor_copy(d_dealt[:].rearrange("p (t c i) -> p c t i", t=PACK, i=4), d_k1[:].rearrange("p (c i t) -> p c t i", t=PACK, i=4))
         b_bank = [bank(f"b{t}", f"b{t}") for t in range(PACK)]
@@ -139,7 +138,7 @@ def tile_picked_cdjointriebgate_none_p_kernel(tc, x_words, x_scales, w1, gn, w2,
             product(b_bank[t], t, d_dealt, ds_dealt, x_two, xs_two)
 
         late = 65536
-        w2_grouped = placed("w2_grouped", [P, PACK * S], BF16, late)
+        w2_grouped = placed("w2_grouped", [P, PACK * S], BF16, first + 1024)
 
         z_rows = sb("z_rows", [P, PACK, S], BF16)
         z_grouped = placed("z_grouped", [P, PACK * S], BF16, late + 4096)
@@ -147,22 +146,28 @@ def tile_picked_cdjointriebgate_none_p_kernel(tc, x_words, x_scales, w1, gn, w2,
         w2_codes, w2_scales, w2_piece = quantize("w2", w2_grouped, 1)
         for t in range(PACK):
             fetch("S", gate_n1[t], gate_win[t], "n1")
+        w2_view = w2_raw[:].rearrange("p j (m t) -> p m j t", t=PACK)
         for t in range(PACK):
             nc.vector.scalar_tensor_tensor(z_rows[:, t, :], y_bank[t][:], gain[:, t:t + 1], gate_n1[t][:], ALU.mult, ALU.mult)
+            if t == 0:
+                nc.vector.tensor_copy(dealt(w2_grouped), w2_view)
             if t == 1:
-                nc.vector.tensor_copy(dealt(w2_grouped), w2_raw[:].rearrange("p j (m t) -> p m j t", t=PACK))
+                w2_piece(0)
         nc.vector.tensor_copy(
             z_grouped[:].rearrange("p (c i t) -> p c t i", t=PACK, i=4),
             z_rows[:].rearrange("p t (c i) -> p c t i", i=4))
-        w2_piece(0)
         z_piece(0)
 
         s_turned = [sb(f"s_turned{t}", [P, S], F32) for t in range(PACK)]
         sum_bank = [None] * PACK
         s_bank = [None] * PACK
-        spot = [late, late + 4096, late + 2048, late]
+        spot = [late + 16384] + [late + 4096 + 64 + 2048 * (t - 2) for t in range(1, PACK)]
         b_n3 = [placed(f"b_n3_{t}", [P, S], F32, spot[t]) for t in range(PACK)]
-        a_n2 = [placed(f"a_n2_{t}", [P, S], F32, spot[t] if t else late + 8192) for t in range(PACK)]
+        a_n2 = [placed(f"a_n2_{t}", [P, S], F32, spot[t] if t else late + 20480) for t in range(PACK)]
+        b_win = [sb(f"b_win{t}", [P, 2 * S], F32) for t in range(PACK)]
+        a_win = [sb(f"a_win{t}", [P, 2 * S], F32) for t in range(PACK)]
+        b_rows = [w[:, :S] for w in b_win]
+        a_rows = [w[:, :S] for w in a_win]
         a_sum = [sb(f"a_sum{t}", [P, S], F32) for t in range(PACK)]
         res = [sb(f"res{t}", [P, S], F32) for t in range(PACK)]
         out_rows = out.rearrange("(p t) j -> p t j", t=PACK)
@@ -199,6 +204,9 @@ def tile_picked_cdjointriebgate_none_p_kernel(tc, x_words, x_scales, w1, gn, w2,
         def add(t, cols=slice(0, S)):
             nc.vector.tensor_tensor(a_sum[t][:, cols], a_bank[t][:, cols], a_n2[t][:, cols], ALU.add)
 
+        def add_in_sbuf(t):
+            nc.gpsimd.tensor_tensor(a_sum[t][:], a_rows[t], a_n2[t][:], ALU.add)
+
         def finish(t, cols=slice(0, S)):
             nc.vector.tensor_tensor(res[t][:, cols], s_bank[t][:, cols], a_sum[t][:, cols], ALU.mult)
             nc.sync.dma_start(out_rows[:, t, cols], res[t][:, cols])
@@ -211,25 +219,25 @@ def tile_picked_cdjointriebgate_none_p_kernel(tc, x_words, x_scales, w1, gn, w2,
         halves = [slice(h * HALF, (h + 1) * HALF) for h in range(2)]
         b_fetch(0, "S")
         b_fetch(1, "V")
+        b_gate(0)
         b_fetch(2, "S")
         a_copy(0, "V")
         a_fetch(0, "V")
-        b_gate(0)
-        a_copy(1, "V")
-        add(0)
         b_fetch(3, "S")
-        a_copy(2, "V")
-        finish(0)
+        a_copy(1, "V")
+        add_in_sbuf(0)
         b_gate(1)
-        a_fetch(1, "S")
         a_copy(3, "V")
+        a_fetch(1, "S")
         a_fetch(3, "V", halves[1])
+        finish(0)
         b_gate(2)
+        a_copy(2, "V")
+        add_in_sbuf(1)
         b_gate(3)
-        add(1)
         a_fetch(3, "S", halves[0])
         finish(1)
-        add(3)
+        add_in_sbuf(3)
         for h in halves:
             a_fetch(2, "S", h)
         finish(3)

from contextlib import ExitStack

import concourse.mybir as mybir

F32 = mybir.dt.float32
BF16 = mybir.dt.bfloat16
I32 = mybir.dt.int32
U32 = mybir.dt.uint32
U16 = mybir.dt.uint16
U8 = mybir.dt.uint8
FP8X4 = mybir.dt.float8_e4m3fn_x4
ACT = mybir.ActivationFunctionType
ALU = mybir.AluOpType

P = 128
PACK = 4
T = 2048
S = 512
HALF = S // 2
FLOPS = 3 * 2 * 512 * 512 * 512


def tile_picked_cdjointriebgate_none_p_kernel(tc, x_words, x_scales, w1, gn, w2, d_words, d_scales, offs, n1, two, k1, n2, n3, out):
    nc = tc.nc
    with ExitStack() as ctx:
        keep = ctx.enter_context(tc.tile_pool(name="keep", bufs=1))
        shared = ctx.enter_context(tc.tile_pool(name="shared", bufs=1))
        psum = ctx.enter_context(tc.psum_pool(name="psum", bufs=1))

        def sb(name, shape, dtype, tag=None):
            return keep.tile(shape, dtype, name=name, tag=tag or name, align_bytes=64)

        def placed(name, shape, dtype, offset):
            return shared.tile(shape, dtype, name=name, align_bytes=64, offset=offset)

        def bank(tag, name):
            return psum.tile([P, S], F32, name=name, tag=tag)

        lists = {name: sb(name + "_list", [P, S // 16], U16) for name in ("offs", "n1", "two", "k1", "n2", "n3")}
        xs_tab = sb("xs_tab", [P, T], U8)
        ds_tab = sb("ds_tab", [P, T], U8)
        w1_raw = [placed(f"w1_raw{h}", [P, PACK, HALF], F32, 32768 + 16384 * h) for h in range(2)]

        w1_rows = w1.rearrange("(p j) c -> p j c", j=PACK)
        xs_rows = x_scales[0].bitcast(I32)
        ds_rows = d_scales[0].bitcast(I32)

        ones = placed("ones", [P, P], F32, 8192 - 256)
        ident = sb("ident", [P, P], F32)
        nc.vector.memset(xs_tab[:].bitcast(I32), 0)
        nc.gpsimd.memset(ds_tab[:].bitcast(I32), 0)
        nc.gpsimd.memset(ones[:], 1.0)
        nc.gpsimd.affine_select(out=ident[:], in_=ones[:], compare_op=ALU.is_equal, fill=0.0, base=0, pattern=[[-1, P]], channel_multiplier=1)
        for name, src in (("offs", offs), ("k1", k1), ("two", two), ("n1", n1), ("n3", n3), ("n2", n2)):
            nc.sync.dma_start(lists[name][:], src)
        for h in range(2):
            nc.sync.dma_start(w1_raw[h][:], w1_rows[:, :, h * HALF:(h + 1) * HALF])
        for i in range(4):
            nc.sync.dma_start(xs_tab[:].bitcast(I32)[i:P:32, :], xs_rows[i:16:4, :])
        nc.sync.dma_start(ds_tab[:].bitcast(I32)[0:P:8, :], ds_rows)
        x_tab = placed("x_tab", [P, T], U32, 0)
        nc.sync.dma_start(x_tab[:].bitcast(I32), x_words[0].rearrange("p n r -> p (n r)").bitcast(I32))

        def pick(name, table, which, dtype, tag=None, offset=None):
            picked = sb(name, [P, S], dtype, tag) if offset is None else placed(name, [P, S], dtype, offset)
            nc.vector.tensor_copy(picked[:], table[:].indirect(lists[which][:]))
            return picked

        def dealt(grouped):
            return grouped[:].rearrange("p (t m j) -> p m j t", t=PACK, j=PACK)

        def quantize(name, grouped, pieces):
            codes = sb(name + "_codes", [P, S], U32)
            scales = sb(name + "_scales", [P, S], U8)

            def piece(i):
                w = S // pieces
                nc.vector.quantize_mx(out=codes[:, i * w:(i + 1) * w].bitcast(FP8X4), scales=scales[:, i * w:(i + 1) * w],
                                      in_=grouped[:, PACK * i * w:PACK * (i + 1) * w])
            return codes, scales, piece

        def product(acc, t, stat, stat_s, mov, mov_s):
            cols = slice(t * P, (t + 1) * P)
            nc.tensor.matmul_mx(out=acc[:], lhsT=stat[:, cols].bitcast(FP8X4), lhsT_scale=stat_s[:, cols],
                                rhs=mov[:].bitcast(FP8X4), rhs_scale=mov_s[:], start=True, stop=True)

        def fetch(engine, dst, window, which, cols=slice(0, S)):
            src = window[:].indirect(lists[which][:, cols.start // 16:cols.stop // 16])
            if engine == "V":
                nc.vector.tensor_copy(dst[:, cols], src)
            else:
                nc.scalar.activation(dst[:, cols], src, ACT.Copy)

        def scaled_copy(engine, dst, src, factor):
            if engine == "V":
                nc.vector.tensor_scalar(dst, src, factor, None, ALU.mult)
            else:
                nc.scalar.activation(dst, src, ACT.Copy, scale=factor)

        base = 16384
        w1_grouped = placed("w1_grouped", [P, PACK * S], BF16, base + 1536)
        w1_views = [w1_raw[h][:].rearrange("p j (m t) -> p m j t", t=PACK) for h in range(2)]
        nc.scalar.copy(dealt(w1_grouped)[:, 0:64], w1_views[0])
        d_tab = placed("d_tab", [P, T], U32, 32768 + 64)
        nc.sync.dma_start(d_tab[:].bitcast(I32), d_words[0].rearrange("p n r -> p (n r)").bitcast(I32))
        gain = placed("gain", [P, PACK], F32, 32768)
        nc.sync.dma_start(gain[:], gn.rearrange("(p t) o -> p (t o)", t=PACK))
        nc.scalar.copy(dealt(w1_grouped)[:, 64:128], w1_views[1])
        w2_raw = placed("w2_raw", [P, PACK, S], F32, 32768 + 16384)
        nc.sync.dma_start(w2_raw[:], w2.rearrange("(p j) c -> p j c", j=PACK))
        xs_offs = pick("xs_offs", xs_tab, "offs", U8)
        ds_k1 = pick("ds_k1", ds_tab, "k1", U8)
        first = 57344
        w1_codes = [placed("w1_codes0", [P, HALF], U32, first), sb("w1_codes1", [P, HALF], U32)]
        w1_scales = [placed("w1_scales0", [P, HALF], U8, first + 1024), sb("w1_scales1", [P, HALF], U8)]
        for h in range(2):
            nc.vector.quantize_mx(out=w1_codes[h][:].bitcast(FP8X4), scales=w1_scales[h][:], in_=w1_grouped[:, h * 1024:(h + 1) * 1024])
        x_offs = pick("x_offs", x_tab, "offs", U32, offset=base)
        y_bank = [bank(f"ya{t}", f"y{t}") for t in range(PACK)]
        gate_win = [sb(f"gate_win{t}", [P, 2 * S], F32) for t in range(PACK)]
        gate = [w[:, :S] for w in gate_win]
        gate_n1 = [sb(f"gate_n1_{t}", [P, S], F32) for t in range(PACK)]
        for t in range(PACK):
            product(y_bank[t], t % 2, w1_codes[t // 2], w1_scales[t // 2], x_offs, xs_offs)
        for t in range(PACK):
            nc.scalar.activation(gate[t], y_bank[t][:], ACT.Sigmoid)
        x_two = pick("x_two", x_tab, "two", U32, offset=base + 3072)
        ds_dealt = placed("ds_dealt", [P, S], U8, first)
        nc.vector.tensor_copy(ds_dealt[:].rearrange("p (t m) -> p t m", t=PACK), ds_k1[:].rearrange("p (m t) -> p t m", t=PACK))
        for i in range(1, 4):
            nc.sync.dma_start(ds_dealt[:].bitcast(I32)[i:P:32, :], ds_dealt[:].bitcast(I32)[8 * i:P:32, :])
        xs_two = pick("xs_two", xs_tab, "two", U8, offset=first + 512)
        d_k1 = pick("d_k1", d_tab, "k1", U32, offset=first + 1024)
        d_dealt = sb("d_dealt", [P, S], U32)
        nc.vector.tensor_copy(d_dealt[:].rearrange("p (t c i) -> p c t i", t=PACK, i=4), d_k1[:].rearrange("p (c i t) -> p c t i", t=PACK, i=4))
        b_bank = [bank(f"b{t}", f"b{t}") for t in range(PACK)]
        for t in range(PACK):
            product(b_bank[t], t, d_dealt, ds_dealt, x_two, xs_two)

        late = 65536
        w2_grouped = placed("w2_grouped", [P, PACK * S], BF16, first + 1024)

        z_rows = sb("z_rows", [P, PACK, S], BF16)
        z_grouped = placed("z_grouped", [P, PACK * S], BF16, late + 4096)
        z_codes, z_scales, z_piece = quantize("z", z_grouped, 1)
        w2_codes, w2_scales, w2_piece = quantize("w2", w2_grouped, 1)
        for t in range(PACK):
            fetch("S", gate_n1[t], gate_win[t], "n1")
        w2_view = w2_raw[:].rearrange("p j (m t) -> p m j t", t=PACK)
        for t in range(PACK):
            nc.vector.scalar_tensor_tensor(z_rows[:, t, :], y_bank[t][:], gain[:, t:t + 1], gate_n1[t][:], ALU.mult, ALU.mult)
            if t == 0:
                nc.vector.tensor_copy(dealt(w2_grouped), w2_view)
            if t == 1:
                w2_piece(0)
        nc.vector.tensor_copy(
            z_grouped[:].rearrange("p (c i t) -> p c t i", t=PACK, i=4),
            z_rows[:].rearrange("p t (c i) -> p c t i", i=4))
        z_piece(0)

        s_turned = [sb(f"s_turned{t}", [P, S], F32) for t in range(PACK)]
        sum_bank = [None] * PACK
        s_bank = [None] * PACK
        spot = [late + 16384] + [late + 4096 + 64 + 2048 * (t - 2) for t in range(1, PACK)]
        b_n3 = [placed(f"b_n3_{t}", [P, S], F32, spot[t]) for t in range(PACK)]
        a_n2 = [placed(f"a_n2_{t}", [P, S], F32, spot[t] if t else late + 20480) for t in range(PACK)]
        b_win = [sb(f"b_win{t}", [P, 2 * S], F32) for t in range(PACK)]
        a_win = [sb(f"a_win{t}", [P, 2 * S], F32) for t in range(PACK)]
        b_rows = [w[:, :S] for w in b_win]
        a_rows = [w[:, :S] for w in a_win]
        a_sum = [sb(f"a_sum{t}", [P, S], F32) for t in range(PACK)]
        res = [sb(f"res{t}", [P, S], F32) for t in range(PACK)]
        out_rows = out.rearrange("(p t) j -> p t j", t=PACK)

        def b_copy(t):
            nc.scalar.activation(b_rows[t], b_bank[t][:], ACT.Copy, scale=0.0625)
            sum_bank[t] = bank(f"b{t}", f"bsum{t}")
            for c in range(PACK):
                cols = slice(c * P, (c + 1) * P)
                nc.tensor.matmul(sum_bank[t][:, cols], b_rows[t][:, cols], ident[:], start=(c == 0), stop=False, is_transpose=True)

        def b_fetch(t, engine):
            fetch(engine, b_n3[t], b_win[t], "n3")
            for c in range(PACK):
                cols = slice(c * P, (c + 1) * P)
                nc.tensor.matmul(sum_bank[t][:, cols], b_n3[t][:, cols], ident[:], start=False, stop=(c == PACK - 1), is_transpose=True)

        def b_gate(t):
            nc.scalar.activation(s_turned[t][:], sum_bank[t][:], ACT.Sigmoid)
            s_bank[t] = bank(f"b{t}", f"s{t}")
            for c in range(PACK):
                cols = slice(c * P, (c + 1) * P)
                nc.tensor.transpose(s_bank[t][:, cols], s_turned[t][:, cols], ident[:])

        def a_copy(t, engine):
            if engine == "V":
                nc.vector.tensor_copy(a_rows[t], a_bank[t][:])
            else:
                nc.scalar.copy(a_rows[t], a_bank[t][:])

        def a_fetch(t, engine, cols=slice(0, S)):
            fetch(engine, a_n2[t], a_win[t], "n2", cols)

        def add(t, cols=slice(0, S)):
            nc.vector.tensor_tensor(a_sum[t][:, cols], a_bank[t][:, cols], a_n2[t][:, cols], ALU.add)

        def add_in_sbuf(t):
            nc.gpsimd.tensor_tensor(a_sum[t][:], a_rows[t], a_n2[t][:], ALU.add)

        def finish(t, cols=slice(0, S)):
            nc.vector.tensor_tensor(res[t][:, cols], s_bank[t][:, cols], a_sum[t][:, cols], ALU.mult)
            nc.sync.dma_start(out_rows[:, t, cols], res[t][:, cols])

        for t in range(PACK):
            b_copy(t)
        a_bank = [bank(f"ya{t}", f"a{t}") for t in range(PACK)]
        for t in range(PACK):
            product(a_bank[t], t, w2_codes, w2_scales, z_codes, z_scales)
        halves = [slice(h * HALF, (h + 1) * HALF) for h in range(2)]
        b_fetch(0, "S")
        b_fetch(1, "V")
        b_gate(0)
        b_fetch(2, "S")
        a_copy(0, "V")
        a_fetch(0, "V")
        b_fetch(3, "S")
        a_copy(1, "V")
        add_in_sbuf(0)
        b_gate(1)
        a_copy(3, "V")
        a_fetch(1, "S")
        a_fetch(3, "V", halves[1])
        finish(0)
        b_gate(2)
        a_copy(2, "V")
        add_in_sbuf(1)
        b_gate(3)
        a_fetch(3, "S", halves[0])
        finish(1)
        add_in_sbuf(3)
        for h in halves:
            a_fetch(2, "S", h)
        finish(3)
        for h in halves:
            add(2, h)
            finish(2, h)
